import numpy as np, ml_dtypes
CORES = [16,17,18,19,32,33,34,35]
N = 8
BF = ml_dtypes.bfloat16
def gentries(a):
    return np.ascontiguousarray(a.reshape(8, 16, -1).transpose(0, 2, 1)).reshape(8, -1)
def gtable(e):
    e = np.asarray(e); return np.ascontiguousarray(e.reshape(8, -1, 16).transpose(0, 2, 1)).reshape(128, -1).astype(np.int32)
A, S, G, M, W = 2048, 128, 2, 4, 2944
def tabs(e):
    return np.stack([gtable(v.reshape(8, -1)) for v in e])
def alleles(rng, ex):
    return np.minimum(np.floor(256 * rng.random((N, 128, 2 * A), dtype=np.float32) ** ex.astype(np.float32)), 255).astype(BF)
def rivals(rng):
    k = (N, 8, G, M, A)
    return np.where(rng.random(k) < 0.5, rng.integers(0, A, k), rng.integers(A, W, k))
def setup_inputs(rng):
    return {"haps": alleles(rng, np.exp2(2 * rng.random((N, 128, 1)) - 1)), "eff": rng.integers(0, 128, (N, 128, 1)).astype(np.float32).astype(BF),
            "dam": tabs(rng.integers(0, A, (N, 8, G, A))), "rival": tabs(rivals(rng)), "gift": tabs(rng.integers(0, A, (N, 8, G, N - 1, S)))}
def setup_inputs_ties(rng):
    d = setup_inputs(rng); e = rng.integers(0, 2, (N, 8, 16, 1))
    d["haps"] = (254 * rng.integers(0, 2, (1, 128, 1)) + rng.integers(0, 2, (N, 128, 2 * A))).astype(np.float32).astype(BF)
    for r in range(N): e[r, rng.permutation(8)[:3]] = 0
    d["eff"] = e.reshape(N, 128, 1).astype(np.float32).astype(BF)
    v = rivals(rng); v[:, :, :, 1] = np.where(rng.random((N, 8, G, A)) < 0.25, v[:, :, :, 0], v[:, :, :, 1])
    d["rival"] = tabs(v); return d
def edge(rng, e, places):
    return np.where(rng.random(e.shape) < 0.5, rng.choice(np.array(places), e.shape), e)
def setup_inputs_ends(rng):
    d = setup_inputs(rng); d["haps"][:, :, :2] = 255; d["haps"][:, :, 2 * A - 2:] = 0
    e = rng.integers(0, 128, (N, 8, 16, 1))
    for r in range(N): e[r, rng.permutation(8)[:4]] = 127
    d["eff"] = e.reshape(N, 128, 1).astype(np.float32).astype(BF)
    d["dam"] = tabs(edge(rng, rng.integers(0, A, (N, 8, G, A)), [0, A - 1])); d["gift"] = tabs(edge(rng, rng.integers(0, A, (N, 8, G, N - 1, S)), [0, A - 1]))
    d["rival"] = tabs(edge(rng, rivals(rng), [0, A - 1] + [A + S * k for k in range(N - 1)] + [A + S * k + S - 1 for k in range(N - 1)])); return d
def setup_inputs_one(rng):
    d = setup_inputs(rng); a = rng.integers(0, A, (N, 8, G, A)); a[:, :, 0] = rng.integers(0, A, (N, 8, 1))
    v = rivals(rng); v[:, :, :, 0] = rng.integers(0, W, (N, 8, G, 1))
    b = np.zeros((N, 8, G, N - 1, S), np.int64); b[:] = rng.integers(0, A, (N, 8, G, N - 1, 1))
    d["dam"] = tabs(a); d["rival"] = tabs(v); d["gift"] = tabs(b); return d
def setup_inputs_guests(rng):
    d = setup_inputs(rng)
    v = np.zeros((N, 8, G, M * A), np.int64); v[:] = np.arange(M * A) % (W - A); d["rival"] = tabs(A + rng.permuted(v, axis=-1))
    a = np.zeros((N, 8, G, A), np.int64); a[:] = np.arange(A); d["dam"] = tabs(rng.permuted(a, axis=-1))
    b = np.zeros((N, 8, G, N - 1, A), np.int64); b[:] = np.arange(A); d["gift"] = tabs(rng.permuted(b, axis=-1)[..., :S]); return d
def setup_inputs_spread(rng):
    d = setup_inputs(rng); d["haps"] = alleles(rng, np.exp2(8 * rng.random((N, 128, 1)) - 4))
    d["eff"] = np.floor(128 * rng.random((N, 128, 1)) ** 4).astype(np.float32).astype(BF)
    def u(m, *k): return np.minimum((m * rng.random(k) ** 3).astype(np.int64), m - 1)
    k = (N, 8, G, M, A)
    d["dam"] = tabs(A - 1 - u(A, N, 8, G, A)); d["gift"] = tabs(u(A, N, 8, G, N - 1, S))
    d["rival"] = tabs(np.where(rng.random(k) < 0.5, u(A, *k), W - 1 - u(W - A, *k))); return d
def check_inputs(d):
    bad = []
    h = d["haps"].astype(np.float32); e = d["eff"].astype(np.float32)
    if not ((h >= 0) & (h <= 255) & (h == np.floor(h))).all(): bad.append("haps: whole numbers from 0 to 255")
    if not ((e >= 0) & (e <= 127) & (e == np.floor(e))).all(): bad.append("eff: whole numbers from 0 to 127")
    for k, top in (("dam", A), ("rival", W), ("gift", A)):
        if not ((d[k] >= 0) & (d[k] < top)).all(): bad.append(k + ": range")
    return bad
def reference(haps, eff, dam, rival, gift):
    h = haps.astype(np.int32).reshape(N, 8, 16, A, 2); e = eff.astype(np.int32).reshape(N, 8, 16, 1)
    dl = np.stack([gentries(a) for a in dam]).reshape(N, 8, G, A)
    rl = np.stack([gentries(a) for a in rival]).reshape(N, 8, G, M, A)
    gl = np.stack([gentries(a) for a in gift]).reshape(N, 8, G, N - 1, S)
    i = np.arange(A); mk = np.arange(16)[:, None]
    for t in range(G):
        new = np.zeros_like(h)
        for r in range(N):
            parts = [h[r]]
            for d in range(N - 1):
                q = (r - 1 - d) % N
                parts.append(np.take_along_axis(h[q], gl[q, :, t, d][:, None, :, None], 2))
            w = np.concatenate(parts, 2)
            v = np.sum(e[r] * (w[..., 0] + w[..., 1]), axis=1)
            best = rl[r, :, t, 0]
            for m in range(1, M):
                c = rl[r, :, t, m]; vb = np.take_along_axis(v, best, 1); vc = np.take_along_axis(v, c, 1)
                best = np.where((vc > vb) | ((vc == vb) & (c > best)), c, best)
            for k, p in enumerate((dl[r, :, t], best)):
                x = (181 * p + 75 * i + 217 * t + 389 * k) & 1023
                s = (x >> 9)[:, None]; c = ((x >> 5) & 15)[:, None]
                side = np.where(mk < c, s, 1 - s)
                both = np.take_along_axis(w, p[:, None, :, None], 2)
                new[r, ..., k] = np.take_along_axis(both, side[..., None], 3)[..., 0]
        h = new
    return {"y": h.reshape(N, 128, 2 * A).astype(BF)}

import numpy as np
from concourse.bass import DstId, RemoteDMATransfer
from concourse.mybir import AluOpType as Op, ActivationFunctionType as Fn

N, A, S, W = 8, 2048, 128, 2944
NG = (N - 1) * S
INV = pow(181, -1, 1024)
BIG = 4096.0
EPT = 2
NTB = 5
HAPCUT = [0, 1024, 2048, 3072, 3584, 4096]
LOADORDER = ["h0", "g", "h1", "h2", "h3", "h4", "d", "r0", "e", "r1"]
BF, F32, I32, U16 = "bfloat16", "float32", "int32", "uint16"


def _sb(n, t):
    return ("sbuf", [128, n], t)


SCRATCH = {
    "hap": _sb(2 * A, BF), "effb": _sb(1, BF), "daml": _sb(256, I32), "rivl": _sb(1024, I32), "gifl": _sb(112, I32),
    "s0": _sb(W, BF), "d0": _sb(W, BF), "s1": _sb(W, BF), "d1": _sb(W, BF), "h1": _sb(W, BF),
    "gs0": _sb(NG, BF), "gd0": _sb(NG, BF), "gs1": _sb(NG, BF), "gd1": _sb(NG, BF),
    "rg0": _sb(4 * A, BF), "rg1": _sb(4 * A, BF),
    "mk00": _sb(A, BF), "mk01": _sb(A, BF), "mk10": _sb(A, BF), "mk11": _sb(A, BF),
    "pr00": _sb(A, BF), "pr01": _sb(A, BF), "pr10": _sb(A, BF), "pr11": _sb(A, BF),
    "g1x": _sb(A, BF), "hg": _sb(A, BF), "yb": _sb(2 * A, BF),
    "mti": _sb(512, I32), "mtab": _sb(1024, BF), "dif": _sb(128, I32), "grp": _sb(8, I32), "gone": _sb(8, F32),
    "gcol": _sb(1, F32), "idn": _sb(512, BF), "wts": _sb(144, BF), "cti": _sb(512, I32), "ct": _sb(512, F32),
    "rst": _sb(256, F32), "mx": _sb(1024, F32),
    "gifu": _sb(112, U16), "rivu": _sb(1024, U16), "pu0": _sb(256, U16), "pu1": _sb(256, U16), "dam2": _sb(128, U16),
    "wi0": _sb(256, I32), "wi1": _sb(256, I32), "wu0": _sb(256, U16), "wu1": _sb(256, U16),
}
for _k in range(8):
    SCRATCH["ps%d" % _k] = ("psum", [128, 512], F32)
LOADS = ["l_gif", "l_eff", "l_h0", "l_h1", "l_h2", "l_h3", "l_h4", "l_dam", "l_r0", "l_r1"]
SEMAPHORES = ["cV", "cA", "cP", "cG", "stored", "sent", "a_s0", "a_d0", "a_s1", "a_d1"] + LOADS

CHUNKS = [[(0, 64, 5), (64, 128, 6)], [(0, 64, 7), (64, 96, 5), (96, 128, 6)]]
APART = [0, 64]
ENGINE_AT = {"tab": 5, "gift": 6, "mask": 5, "riv": 4, "fin": 3, "gam": 5}


def steps():
    p = [("ct", 0), ("gidx", 0), ("ct", 1), ("gidx", 1)]
    for j in range(3):
        p.append(("tab", "s", 0, 512 * j, 512 * j + 512, "A"))
        p.append(("tab", "d", 0, 512 * j, 512 * j + 512, "A"))
    p.extend([("tab", "s", 0, 1536, 1792, "A"), ("tab", "s", 0, 1792, 2048, "V")])
    for t in range(2):
        p.extend([("gift", "s", t, 0, 0, 2, "V"), ("gift", "s", t, 0, 1, 2, "A"), ("send", "s", t, 0)])
        p.extend([("gift", "s", t, 1, 0, 2, "V"), ("gift", "s", t, 1, 1, 2, "A"), ("send", "s", t, 1)])
        if t == 0:
            p.append(("tab", "d", 0, 1536, 2048, "A"))
            for u in range(2):
                p.extend(("didx", u, k) for k in range(5 - u))
                p.extend(("ridx", u, k) for k in range(4))
            p.append(("wts",))
        else:
            p.extend(("tab", "d", 1, 512 * j, 512 * j + 512, "A") for j in range(4))
        p.extend([("gift", "d", t, 0, 0, 1, "A"), ("gift", "d", t, 1, 0, 1, "A"), ("send", "d", t, 2)])
        for a in range(0, 128, 32):
            p.extend([("mask", 0, t, a, a + 32, "A"), ("prod", 0, t, a, a + 32), ("gam", 0, t, a, a + 32, "V")])
        if t == 1:
            p.extend([("tab", "h", 1, A, A + 512, "A"), ("tab", "h", 1, A + 512, W, "A")])
        for a, c, vb in CHUNKS[t]:
            p.extend(("riv", t, u, u + 16, "A", vb, a) for u in range(a, c, 16))
            p.extend(("sel", t, a, c, vb, k) for k in range(8))
            for u in range(a, c, 32):
                cuts = [(u, u + 16), (u + 16, u + 32)] if (t, u) == (1, 96) else [(u, u + 32)]
                p.extend(("mask", 1, t, v, w, "A") for v, w in cuts)
                p.extend(("prod", 1, t, v, w) for v, w in cuts)
                p.extend(("gam", 1, t, v, w, "a" if u >= APART[t] else "V") for v, w in cuts)
                if t == 1:
                    if u >= APART[t]:
                        p.extend(("fin", v, w, "A") for v, w in cuts)
                    p.extend(("store", v, w) for v, w in cuts)
        if t == 0:
            p.extend(("tab", "s", 1, 512 * j, 512 * j + 512, "A") for j in range(3))
            p.extend([("tab", "s", 1, 1536, 1792, "A"), ("tab", "s", 1, 1792, 2048, "V")])
    return p


ORDER = [1,4,3,5,7,2,0,6,8,19,10,11,13,12,15,20,16,31,36,9,26,27,28,18,21,46,24,14,43,37,49,22,23,50,35,34,40,25,38,
         51,44,29,41,47,42,48,30,32,17,33,53,54,52,55,45,71,56,73,57,58,59,60,39,72,70,63,66,69,61,62,64,65,74,75,76,
         77,78,67,81,106,79,80,82,84,68,85,83,86,87,88,89,115,90,92,91,94,99,97,93,109,95,112,96,100,102,101,104,107,
         103,116,113,98,121,108,123,120,122,110,117,114,140,111,105,124,125,126,127,141,142,128,156,143,144,129,155,
         145,130,136,131,146,149,147,157,148,150,119,118,152,158,159,137,151,138,160,161,132,153,164,162,169,133,163,
         165,139,134,154,166,170,135,167,171,168,172,173,174]
ENGINES = ("....AAAAVAAAAV.AA.A..................AA.A.VA.VA.VV.VAAVV........V.AA.AAAAA........A.AV.AAAVVVVA.VA.AVVVAA."
           "A.VA.VA.VA.VAAAAVV........A.V.A.V.AA........A.AA.AA........AA..AAAV..")


def planned():
    base, out = steps(), []
    for i in ORDER:
        k = list(base[i])
        if k[0] in ENGINE_AT and not (k[0] == "gam" and k[5] == "V"):
            k[ENGINE_AT[k[0]]] = ENGINES[i].lower() if k[0] == "gam" else ENGINES[i]
        out.append(tuple(k))
    return out


PLAN = planned()


def build(g, core, T, topo, plan):
    rank = T.rank_of(core)
    Qs = {"V": g.vector, "A": g.scalar, "P": g.tensor, "G": g, "S": g.sync}
    ops = []
    tok = [-1]

    def ap(v):
        return T[v[0]][:, v[1]:v[2]] if len(v) == 3 else T[v[0]][:, v[1]:v[2]:v[3]]

    def ind(win, off):
        return ap(win).indirect(ap(off))

    def add(q, fn, reads, writes, sem=None, n=16):
        ops.append({"q": q, "fn": fn, "r": reads, "w": writes, "sem": sem, "n": n, "tok": tok[0]})

    def load(q, sem, dst, src):
        add(q, lambda: Qs[q].dma_start(ap(dst), src), [], [dst], sem)

    def ts(out, a, s1, s2, o0, o1=None):
        rd = [a] + [x for x in (s1, s2) if isinstance(x, tuple)]
        x1 = ap(s1) if isinstance(s1, tuple) else s1
        x2 = ap(s2) if isinstance(s2, tuple) else s2
        if o1 is None:
            add("V", lambda: g.vector.tensor_scalar(ap(out), ap(a), x1, None, o0), rd, [out])
        else:
            add("V", lambda: g.vector.tensor_scalar(ap(out), ap(a), x1, x2, o0, o1), rd, [out])

    def cp(out, a):
        add("V", lambda: g.vector.tensor_copy(ap(out), ap(a)), [a], [out])

    def tt(out, a, b, o):
        add("V", lambda: g.vector.tensor_tensor(ap(out), ap(a), ap(b), o), [a, b], [out])

    def fill(out, c):
        add("V", lambda: g.vector.memset(ap(out), c), [], [out])

    def iota(out, pat, base, ch):
        add("G", lambda: g.iota(ap(out), pat, base, ch), [], [out])

    def affine(e, out, a, scale, bias, off=None):
        rd = [a] if off is None else [a, off]

        def fn():
            src = ap(a) if off is None else ind(a, off)
            if e == "A":
                return g.scalar.activation(ap(out), src, Fn.Identity, bias=float(bias), scale=float(scale))
            if scale == 1 and bias == 0:
                return g.vector.tensor_copy(ap(out), src)
            return g.vector.tensor_scalar(ap(out), src, float(scale), float(bias), Op.mult, Op.add)
        add(e, fn, rd, [out])

    def gtt(out, win, off, b, o):
        add("V", lambda: g.vector.tensor_tensor(ap(out), ind(win, off), ap(b), o), [win, off, b], [out])

    def mm(out, terms):
        for k, (w, x) in enumerate(terms):
            add("P", lambda w=w, x=x, k=k: g.tensor.matmul(ap(out), ap(w), ap(x), k == 0, k == len(terms) - 1), [w, x], [out])

    ONE, NEG, HALF, NEG2 = ("idn", 0, 128), ("idn", 128, 256), ("idn", 256, 384), ("idn", 384, 512)
    bank = [0]
    apart = [(k[3], k[4]) for k in plan if k[0] == "gam" and k[1] == 1 and k[2] == 0 and k[5] != "V"]

    def nextbank():
        bank[0] += 1
        return "ps%d" % ((bank[0] - 1) % NTB)

    def table(kind, t, a, b, e):
        ps = (nextbank(), 0, b - a)
        if kind == "h":
            mm(ps, [(ONE, ("s1", a, b)), (NEG, ("d1", a, b))])
            affine(e, ("h1", a, b), ps, 0.5, 127.5)
        elif t == 0:
            mm(ps, [(ONE if kind == "s" else NEG, ("hap", 2 * a, 2 * b, 2)), (ONE, ("hap", 2 * a + 1, 2 * b, 2))])
            affine(e, (kind + "0", a, b), ps, 1, -255 if kind == "s" else 0)
        elif kind == "d":
            mm(ps, [(ONE, ("s1", a, b)), (NEG2, ("h1", a, b))])
            affine(e, ("d1", a, b), ps, 1, 255)
        else:
            terms = [(ONE, ("h1", a, b)), (HALF, ("g1x", a, b))]
            if any(16 * u <= a and b <= 16 * v for u, v in apart):
                terms.append((HALF, ("pr01", a, b)))
            mm(ps, terms)
            affine(e, ("s1", a, b), ps, 1, -127.5)

    dests = [T.cores[(rank + 1 + d) % N] for d in range(N - 1)]
    far = [d for d in range(N - 1) if topo.chip(dests[d]) != topo.chip(core)]
    order = far + [d for d in range(N - 1) if d not in far]
    parts = [(0, len(far)), (len(far), N - 1), (0, N - 1)]
    masks, used = {}, []
    for d in order:
        free = [e for e in topo.engines(core, dests[d]) if e not in used][:EPT]
        used.extend(free)
        masks[d] = sum(1 << e for e in free)
    nsent = [0]

    def gifts(kind, t, part, h, nh, e):
        lo, hi = 8 * parts[part][0], 8 * parts[part][1]
        a, b = lo + (hi - lo) * h // nh, lo + (hi - lo) * (h + 1) // nh
        affine(e, ("g%s%d" % (kind, t), 16 * a, 16 * b), ("%s%d" % (kind, t), 0, A), 1, 0, ("gifu", 56 * t + a, 56 * t + b))

    def send(kind, t, part):
        tab, src = "%s%d" % (kind, t), "g%s%d" % (kind, t)
        lo, hi = parts[part]

        def fn():
            tr = []
            for k in range(lo, hi):
                d = order[k]
                rid, pid = topo.addr(dests[d])[:2]
                tr.append(RemoteDMATransfer(dst_ids=[DstId(rid=rid, pnc=pid)], dma_engine_mask=masks[d], remote_sem=T.sem["a_" + tab],
                                            src=ap((src, S * k, S * k + S)), dst=ap((tab, A + S * d, A + S * d + S))))
            return g.remote_dma_fused(tr, local_sem=T.sem.sent)
        add("G", fn, [(src, S * lo, S * hi)], [], "sent", 0)
        nsent[0] += EPT * (hi - lo)
        if hi == N - 1:
            add(None, None, [], [(tab, A, W)], "a_" + tab, EPT * (N - 1))

    def windex(b, t, a, c, p, step):
        lo, hi = 128 * t + a, 128 * t + c
        wi, wu = ("wi%d" % b, lo, hi), ("wu%d" % b, lo, hi)
        if step == 0:
            tt(wi, p, ("ct", 256 * b + lo, 256 * b + hi), Op.add)
        elif step == 1:
            ts(wi, wi, 1023, None, Op.bitwise_and)
        elif step == 2:
            cp(wu, wi)
        else:
            cp(("pu%d" % b, lo, hi), p)

    def damidx(t, step):
        p = ("daml", 128 * t, 128 * t + 128)
        if step < 4:
            windex(0, t, 0, 128, p, step)
        else:
            ts(("dam2", 0, 128), p, 2.0, None, Op.mult)

    def rividx(t, k):
        cp(("rivu", 512 * t + k, 512 * t + 512, 4), ("rivl", 512 * t + 128 * k, 512 * t + 128 * k + 128))

    def mask(b, t, a, c, e):
        two = t == 0 and b == 1
        affine(e, ("mk%d%d" % (t, b), 16 * a, 16 * c), ("mtab", 0, 1024), 2 if two else 1, -1 if two else 0,
               ("wu%d" % b, 128 * t + a, 128 * t + c))

    def prod(b, t, a, c):
        gtt(("pr%d%d" % (t, b), 16 * a, 16 * c), ("d%d" % t, 0, W if b else A), ("pu%d" % b, 128 * t + a, 128 * t + c),
            ("mk%d%d" % (t, b), 16 * a, 16 * c), Op.mult)

    def gam(b, t, a, c, e):
        pr, off = ("pr%d%d" % (t, b), 16 * a, 16 * c), ("pu%d" % b, 128 * t + a, 128 * t + c)
        if e != "V":
            affine(e.upper(), ("hg" if t else "g1x", 16 * a, 16 * c), ("h1" if t else "s0", 0, W), 1, 0, off)
        elif t == 1:
            gtt(("yb", 32 * a + b, 32 * c, 2), ("h1", 0, W if b else A), off, pr, Op.add)
        elif b == 0:
            gtt(("h1", 16 * a, 16 * c), ("hap", 0, 2 * A), ("dam2", a, c), pr, Op.add)
        else:
            gtt(("g1x", 16 * a, 16 * c), ("s0", 0, W), off, pr, Op.add)

    def fin(a, c, e):
        ps = (nextbank(), 0, 16 * (c - a))
        mm(ps, [(ONE, ("hg", 16 * a, 16 * c)), (ONE, ("pr11", 16 * a, 16 * c))])
        affine(e, ("yb", 32 * a + 1, 32 * c, 2), ps, 1, 0)

    def rivals(t, a, c, e, vb, a0):
        rg = "rg%d" % t
        affine(e, (rg, 64 * a, 64 * c), ("s%d" % t, 0, W), 1, 0, ("rivu", 512 * t + 4 * a, 512 * t + 4 * c))
        mm(("ps%d" % vb, 4 * (a - a0), 4 * (c - a0)), [(("wts", 15 - q, 143 - q), (rg, 64 * a + q, 64 * c, 16)) for q in range(16)])

    def scan(out, v, n):
        add("V", lambda: g.vector.tensor_tensor_scan(ap(out), ap(("rst", 0, n)), ap(v), 0.0, Op.add, Op.max), [("rst", 0, n), v], [out])

    def select(t, a, c, vb, step):
        n, pb, m0 = 4 * (c - a), "ps%d" % vb, 512 * t + 4 * a
        if step == 0:
            scan(("mx", m0, m0 + n), (pb, 0, n), n)
        elif step == 1:
            for k in range(4):
                tt((pb, k, n, 4), (pb, k, n, 4), ("mx", m0 + 3, m0 + n, 4), Op.subtract)
        elif step == 2:
            for k in range(4):
                r0 = 512 * t + 128 * k
                tt((pb, k, n, 4), (pb, k, n, 4), ("rivl", r0 + a, r0 + c), Op.add)
        elif step == 3:
            scan((pb, 256, 256 + n), (pb, 0, n), n)
        else:
            windex(1, t, a, c, (pb, 259, 256 + n, 4), step - 4)

    nst = [0]

    def store(a, c):
        add("S", lambda: g.sync.dma_start(T.y[:, 32 * a:32 * c], ap(("yb", 32 * a, 32 * c))), [("yb", 32 * a, 32 * c)], [], "stored")
        nst[0] += 16

    def weights():
        ts(("wts", 15, 143, 16), ("gone", 0, 8), ("effb", 0, 1), None, Op.mult)

    def const(b):
        ts(("ct", 256 * b, 256 * b + 256), ("cti", 256 * b, 256 * b + 256), ("gcol", 0, 1), None, Op.add)

    def giftidx(t):
        k = 0
        while k < N - 1:
            e = k + 1
            while e < N - 1 and order[e] == order[e - 1] + 1:
                e += 1
            cp(("gifu", 56 * t + 8 * k, 56 * t + 8 * e), ("gifl", 56 * t + 8 * order[k], 56 * t + 8 * (order[k] + e - k)))
            k = e

    for nm in LOADORDER:
        if nm[0] == "h":
            j = int(nm[1])
            load("A" if j % 2 == 0 else "S", "l_h%d" % j, ("hap", HAPCUT[j], HAPCUT[j + 1]), T.haps[:, HAPCUT[j]:HAPCUT[j + 1]])
        elif nm == "g":
            load("S", "l_gif", ("gifl", 0, 112), T.gift[:])
        elif nm == "e":
            load("S", "l_eff", ("effb", 0, 1), T.eff[:])
        elif nm == "d":
            load("S", "l_dam", ("daml", 0, 256), T.dam[:])
        else:
            j = int(nm[1])
            load("S", "l_r%d" % j, ("rivl", 512 * j, 512 * j + 512), T.rival[:, 512 * j:512 * j + 512])
    iota(("dif", 0, 128), [[-1, 128]], 0, 1)
    iota(("mti", 0, 512), [[181, 512]], 8192 - 32, -32)
    iota(("cti", 0, 512), [[INV * 389 % 1024, 2], [INV * 217 % 1024, 2], [INV * 1200 % 1024, 128]], 0, INV * 75 % 1024)
    fill(("wts", 0, 144), 0.0)
    fill(("rst", 0, 256), 0.0)
    ts(ONE, ("dif", 0, 128), 0.0, 1.0, Op.is_equal, Op.mult)
    ts(NEG, ("dif", 0, 128), 0.0, -1.0, Op.is_equal, Op.mult)
    ts(("grp", 0, 8), ("dif", 0, 128, 16), 4, None, Op.arith_shift_right)
    fill(("rst", 0, 256, 4), -1e12)
    ts(HALF, ("dif", 0, 128), 0.0, 0.5, Op.is_equal, Op.mult)
    ts(NEG2, ("dif", 0, 128), 0.0, -2.0, Op.is_equal, Op.mult)
    ts(("gone", 0, 8), ("grp", 0, 8), 0.0, BIG, Op.is_equal, Op.mult)
    ts(("gcol", 0, 1), ("grp", 0, 1), float(INV * (512 - 1200) % 1024), None, Op.mult)
    ts(("mti", 0, 512), ("mti", 0, 512), 9, 1, Op.arith_shift_right, Op.bitwise_and)
    cp(("mtab", 0, 512), ("mti", 0, 512))
    ts(("mtab", 512, 1024), ("mtab", 0, 512), -1.0, 1.0, Op.mult, Op.add)
    calls = {"tab": table, "gift": gifts, "send": send, "didx": damidx, "ridx": rividx, "mask": mask, "prod": prod,
             "gam": gam, "fin": fin, "riv": rivals, "sel": select, "store": store, "wts": weights, "ct": const, "gidx": giftidx}
    for i, k in enumerate(plan):
        tok[0] = i
        calls[k[0]](*k[1:])
    return ops, nsent[0], nst[0]


def depend(ops):
    cols = {n: v[1][1] for n, v in SCRATCH.items()}
    lastw = {n: np.full(c, -1) for n, c in cols.items()}
    lastr = {n: {} for n in cols}
    lastp = {n: {} for n in cols if SCRATCH[n][0] == "psum"}
    for i, o in enumerate(ops):
        q, dep = o["q"], set()
        for v in o["r"] + o["w"]:
            dep.update(int(x) for x in np.unique(lastw[v[0]][slice(*v[1:])]))
            if v[0] in lastp:
                dep.update(x for e, x in lastp[v[0]].items() if e != q)
        for v in o["w"]:
            for a in lastr[v[0]].values():
                dep.update(int(x) for x in np.unique(a[slice(*v[1:])]))
        dep.discard(-1)
        for v in o["r"]:
            lastr[v[0]].setdefault(q, np.full(cols[v[0]], -1))[slice(*v[1:])] = i
        for v in o["w"]:
            lastw[v[0]][slice(*v[1:])] = i
        for v in o["r"] + o["w"]:
            if v[0] in lastp:
                lastp[v[0]][q] = i
        o["dep"] = dep


def rank_program(g, core, T, topo):
    if T.rank_of(core) is None:
        return
    Qs = {"V": g.vector, "A": g.scalar, "P": g.tensor, "G": g, "S": g.sync}
    ops, nsent, nstored = build(g, core, T, topo, PLAN)
    depend(ops)
    seq, known = {q: 0 for q in Qs}, {q: {} for q in Qs}
    for o in ops:
        q = o["q"]
        o["waits"] = []
        if q is None:
            o["key"], o["seq"], o["clock"] = o["sem"], 1, {}
            continue
        kn = known[q]
        for j in sorted(o["dep"], reverse=True):
            p = ops[j]
            if p["q"] == "P" and q == "P":
                continue
            if kn.get(p["key"], 0) < p["seq"]:
                o["waits"].append(j)
                p["used"] = True
                for k2, v2 in p["clock"].items():
                    kn[k2] = max(kn.get(k2, 0), v2)
                kn[p["key"]] = p["seq"]
        if o["sem"] is None:
            seq[q] += 1
            o["key"], o["seq"] = q, seq[q]
        else:
            o["key"], o["seq"] = o["sem"], 1
        o["clock"] = dict(kn)
    count = {q: 0 for q in Qs}
    for o in ops:
        q = o["q"]
        if q is None:
            continue
        for j in o["waits"]:
            p = ops[j]
            if p["sem"] is None:
                Qs[q].wait_ge(T.sem["c" + p["q"]], p["count"])
            else:
                Qs[q].wait_ge(T.sem[p["sem"]], p["n"])
        ins = o["fn"]()
        if o["sem"] is None:
            if o.get("used"):
                count[q] += 1
                o["count"] = count[q]
                ins.then_inc(T.sem["c" + q], 1)
        elif o["n"]:
            ins.then_inc(T.sem[o["sem"]], 16)
    g.wait_ge(T.sem.sent, nsent)
    g.sync.wait_ge(T.sem.stored, nstored)
